import numpy as np
import ml_dtypes

BF16 = ml_dtypes.bfloat16


def bf(x):
    return np.asarray(x, np.float32).astype(BF16)


def f32(x):
    return np.asarray(x, np.float32)


def f64(x):
    return np.asarray(x).astype(np.float64)


def striped(idx):
    return np.tile(idx.reshape(-1, 16).T, (8, 1))


S, K, M, N = 2048, 128, 128, 2048


def setup_inputs():
    return {"table": bf(np.random.standard_normal((K, S))), "w": bf(np.random.standard_normal((K, M)) / np.sqrt(K)), "b": f32(0.5 * np.random.standard_normal((M, 1))), "offs": striped(np.random.permutation(S))}


def reference(table, w, b, offs):
    idx = offs[:16].T.reshape(-1)
    x = f64(table)[:, idx]
    y = f64(w).T @ x
    return np.maximum(y + f64(b), 0.0)

@@ -1,0 +1,45 @@
+import concourse.mybir as mybir
+
+BF16, F32, U16 = mybir.dt.bfloat16, mybir.dt.float32, mybir.dt.uint16
+RELU = mybir.ActivationFunctionType.Relu
+ADD, MAX = mybir.AluOpType.add, mybir.AluOpType.max
+
+P = 128
+TOKENS = 2048
+PIECE = 512
+PER_COLUMN = 16
+
+FLOPS = 2 * P * P * TOKENS
+
+
+def tile_gather_matmul_kernel(tc, table, w, b, offs, out):
+    nc = tc.nc
+    pieces = TOKENS // PIECE
+    with (
+        tc.tile_pool(name="held", bufs=1) as held,
+        tc.tile_pool(name="results", bufs=pieces) as results,
+        tc.psum_pool(name="banks", bufs=pieces) as banks,
+    ):
+        offsets = held.tile([P, TOKENS // PER_COLUMN], U16, name="offsets")
+        nc.sync.dma_start(offsets[:], offs)
+        tokens = held.tile([P, TOKENS], BF16, name="tokens")
+        nc.scalar.dma_start(tokens[:], table)
+        weights = held.tile([P, P], BF16, name="weights")
+        nc.sync.dma_start(weights[:], w)
+        bias = held.tile([P, 1], F32, name="bias")
+        nc.sync.dma_start(bias[:], b)
+
+        for piece in range(pieces):
+            first = piece * PIECE
+            bank = banks.tile([P, PIECE], F32, name="bank")
+            picked = tokens[:].indirect(
+                offsets[:, first // PER_COLUMN : (first + PIECE) // PER_COLUMN]
+            )
+            nc.tensor.matmul(bank[:], weights[:], picked, start=True, stop=True)
+
+            result = results.tile([P, PIECE], F32, name="result")
+            if piece % 2 == 0:
+                nc.scalar.activation(result[:], bank[:], RELU, bias=bias[:, 0:1])
+            else:
+                nc.vector.tensor_scalar(result[:], bank[:], bias[:, 0:1], 0.0, ADD, MAX)
+            nc.sync.dma_start(out[:, first : first + PIECE], result[:])

@@ -6,8 +6,10 @@ ADD, MAX = mybir.AluOpType.add, mybir.AluOpType.max
 
 P = 128
 TOKENS = 2048
+BANK = 512
 PIECE = 512
 PER_COLUMN = 16
+WARM_UPS = 24
 
 FLOPS = 2 * P * P * TOKENS
 
@@ -18,7 +20,8 @@ def tile_gather_matmul_kernel(tc, table, w, b, offs, out):
     with (
         tc.tile_pool(name="held", bufs=1) as held,
         tc.tile_pool(name="results", bufs=pieces) as results,
-        tc.psum_pool(name="banks", bufs=pieces) as banks,
+        tc.psum_pool(name="idle_bank", bufs=1) as idle_bank,
+        tc.psum_pool(name="banks", bufs=4) as banks,
     ):
         offsets = held.tile([P, TOKENS // PER_COLUMN], U16, name="offsets")
         nc.sync.dma_start(offsets[:], offs)
@@ -28,6 +31,14 @@ def tile_gather_matmul_kernel(tc, table, w, b, offs, out):
         nc.sync.dma_start(weights[:], w)
         bias = held.tile([P, 1], F32, name="bias")
         nc.sync.dma_start(bias[:], b)
+
+        zeros = held.tile([P, P], BF16, name="zeros")
+        nc.gpsimd.memset(zeros[:], 0.0)
+        unused = idle_bank.tile([P, P], F32, name="unused")
+        for unused_turn in range(WARM_UPS):
+            nc.tensor.matmul(unused[:], zeros[:], zeros[:], start=True, stop=True)
+        early = held.tile([P, 1], BF16, name="early")
+        nc.scalar.activation(early[:], zeros[:, 0:1], RELU)
 
         for piece in range(pieces):
             first = piece * PIECE

@@ -6,10 +6,9 @@ ADD, MAX = mybir.AluOpType.add, mybir.AluOpType.max
 
 P = 128
 TOKENS = 2048
-BANK = 512
-PIECE = 512
+PIECE = 256
 PER_COLUMN = 16
-WARM_UPS = 24
+BANKS = 8
 
 FLOPS = 2 * P * P * TOKENS
 
@@ -17,26 +16,24 @@ FLOPS = 2 * P * P * TOKENS
 def tile_gather_matmul_kernel(tc, table, w, b, offs, out):
     nc = tc.nc
     pieces = TOKENS // PIECE
+    half = TOKENS // 2
     with (
         tc.tile_pool(name="held", bufs=1) as held,
         tc.tile_pool(name="results", bufs=pieces) as results,
-        tc.psum_pool(name="idle_bank", bufs=1) as idle_bank,
-        tc.psum_pool(name="banks", bufs=4) as banks,
+        tc.psum_pool(name="banks", bufs=BANKS) as banks,
     ):
         offsets = held.tile([P, TOKENS // PER_COLUMN], U16, name="offsets")
-        nc.sync.dma_start(offsets[:], offs)
         tokens = held.tile([P, TOKENS], BF16, name="tokens")
-        nc.scalar.dma_start(tokens[:], table)
         weights = held.tile([P, P], BF16, name="weights")
-        nc.sync.dma_start(weights[:], w)
         bias = held.tile([P, 1], F32, name="bias")
-        nc.sync.dma_start(bias[:], b)
+        nc.sync.dma_start(offsets[:], offs)
+        nc.scalar.dma_start(tokens[:, 0:half], table[:, 0:half])
+        nc.sync.dma_start(weights[:], w)
+        nc.sync.dma_start(tokens[:, half:TOKENS], table[:, half:TOKENS])
+        nc.scalar.dma_start(bias[:], b)
 
-        zeros = held.tile([P, P], BF16, name="zeros")
-        nc.gpsimd.memset(zeros[:], 0.0)
-        unused = idle_bank.tile([P, P], F32, name="unused")
-        for unused_turn in range(WARM_UPS):
-            nc.tensor.matmul(unused[:], zeros[:], zeros[:], start=True, stop=True)
+        zeros = held.tile([P, 1], BF16, name="zeros")
+        nc.vector.memset(zeros[:], 0.0)
         early = held.tile([P, 1], BF16, name="early")
         nc.scalar.activation(early[:], zeros[:, 0:1], RELU)
 

@@ -6,7 +6,7 @@ ADD, MAX = mybir.AluOpType.add, mybir.AluOpType.max
 
 P = 128
 TOKENS = 2048
-PIECE = 256
+PIECES = (128, 128, 256, 512, 512, 256, 128, 128)
 PER_COLUMN = 16
 BANKS = 8
 
@@ -15,11 +15,11 @@ FLOPS = 2 * P * P * TOKENS
 
 def tile_gather_matmul_kernel(tc, table, w, b, offs, out):
     nc = tc.nc
-    pieces = TOKENS // PIECE
+    assert sum(PIECES) == TOKENS
     half = TOKENS // 2
     with (
         tc.tile_pool(name="held", bufs=1) as held,
-        tc.tile_pool(name="results", bufs=pieces) as results,
+        tc.tile_pool(name="results", bufs=len(PIECES)) as results,
         tc.psum_pool(name="banks", bufs=BANKS) as banks,
     ):
         offsets = held.tile([P, TOKENS // PER_COLUMN], U16, name="offsets")
@@ -37,17 +37,18 @@ def tile_gather_matmul_kernel(tc, table, w, b, offs, out):
         early = held.tile([P, 1], BF16, name="early")
         nc.scalar.activation(early[:], zeros[:, 0:1], RELU)
 
-        for piece in range(pieces):
-            first = piece * PIECE
-            bank = banks.tile([P, PIECE], F32, name="bank")
+        first = 0
+        for piece, width in enumerate(PIECES):
+            bank = banks.tile([P, width], F32, name="bank")
             picked = tokens[:].indirect(
-                offsets[:, first // PER_COLUMN : (first + PIECE) // PER_COLUMN]
+                offsets[:, first // PER_COLUMN : (first + width) // PER_COLUMN]
             )
             nc.tensor.matmul(bank[:], weights[:], picked, start=True, stop=True)
 
-            result = results.tile([P, PIECE], F32, name="result")
+            result = results.tile([P, width], F32, name="result")
             if piece % 2 == 0:
                 nc.scalar.activation(result[:], bank[:], RELU, bias=bias[:, 0:1])
             else:
                 nc.vector.tensor_scalar(result[:], bank[:], bias[:, 0:1], 0.0, ADD, MAX)
-            nc.sync.dma_start(out[:, first : first + PIECE], result[:])
+            nc.sync.dma_start(out[:, first : first + width], result[:])
+            first += width

@@ -6,20 +6,22 @@ ADD, MAX = mybir.AluOpType.add, mybir.AluOpType.max
 
 P = 128
 TOKENS = 2048
-PIECES = (128, 128, 256, 512, 512, 256, 128, 128)
+PIECE = 256
 PER_COLUMN = 16
-BANKS = 8
+BANKS = 7
+WARM_UPS = 16
 
 FLOPS = 2 * P * P * TOKENS
 
 
 def tile_gather_matmul_kernel(tc, table, w, b, offs, out):
     nc = tc.nc
-    assert sum(PIECES) == TOKENS
+    pieces = TOKENS // PIECE
     half = TOKENS // 2
     with (
         tc.tile_pool(name="held", bufs=1) as held,
-        tc.tile_pool(name="results", bufs=len(PIECES)) as results,
+        tc.tile_pool(name="results", bufs=pieces) as results,
+        tc.psum_pool(name="idle_bank", bufs=1) as idle_bank,
         tc.psum_pool(name="banks", bufs=BANKS) as banks,
     ):
         offsets = held.tile([P, TOKENS // PER_COLUMN], U16, name="offsets")
@@ -32,23 +34,26 @@ def tile_gather_matmul_kernel(tc, table, w, b, offs, out):
         nc.sync.dma_start(tokens[:, half:TOKENS], table[:, half:TOKENS])
         nc.scalar.dma_start(bias[:], b)
 
-        zeros = held.tile([P, 1], BF16, name="zeros")
-        nc.vector.memset(zeros[:], 0.0)
+        zeros = held.tile([P, P], BF16, name="zeros")
+        nc.gpsimd.memset(zeros[:], 0.0)
         early = held.tile([P, 1], BF16, name="early")
         nc.scalar.activation(early[:], zeros[:, 0:1], RELU)
 
-        first = 0
-        for piece, width in enumerate(PIECES):
-            bank = banks.tile([P, width], F32, name="bank")
+        unused = idle_bank.tile([P, P], F32, name="unused")
+        for turn in range(WARM_UPS):
+            nc.tensor.matmul(unused[:], zeros[:], zeros[:], start=True, stop=True)
+
+        for piece in range(pieces):
+            first = piece * PIECE
+            bank = banks.tile([P, PIECE], F32, name="bank")
             picked = tokens[:].indirect(
-                offsets[:, first // PER_COLUMN : (first + width) // PER_COLUMN]
+                offsets[:, first // PER_COLUMN : (first + PIECE) // PER_COLUMN]
             )
             nc.tensor.matmul(bank[:], weights[:], picked, start=True, stop=True)
 
-            result = results.tile([P, width], F32, name="result")
+            result = results.tile([P, PIECE], F32, name="result")
             if piece % 2 == 0:
                 nc.scalar.activation(result[:], bank[:], RELU, bias=bias[:, 0:1])
             else:
                 nc.vector.tensor_scalar(result[:], bank[:], bias[:, 0:1], 0.0, ADD, MAX)
-            nc.sync.dma_start(out[:, first : first + width], result[:])
-            first += width
+            nc.sync.dma_start(out[:, first : first + PIECE], result[:])

@@ -6,7 +6,8 @@ ADD, MAX = mybir.AluOpType.add, mybir.AluOpType.max
 
 P = 128
 TOKENS = 2048
-PIECE = 256
+PIECE = 128
+STORE = 2 * PIECE
 PER_COLUMN = 16
 BANKS = 7
 WARM_UPS = 16
@@ -16,11 +17,10 @@ FLOPS = 2 * P * P * TOKENS
 
 def tile_gather_matmul_kernel(tc, table, w, b, offs, out):
     nc = tc.nc
-    pieces = TOKENS // PIECE
     half = TOKENS // 2
     with (
         tc.tile_pool(name="held", bufs=1) as held,
-        tc.tile_pool(name="results", bufs=pieces) as results,
+        tc.tile_pool(name="results", bufs=TOKENS // STORE) as results,
         tc.psum_pool(name="idle_bank", bufs=1) as idle_bank,
         tc.psum_pool(name="banks", bufs=BANKS) as banks,
     ):
@@ -43,17 +43,19 @@ def tile_gather_matmul_kernel(tc, table, w, b, offs, out):
         for turn in range(WARM_UPS):
             nc.tensor.matmul(unused[:], zeros[:], zeros[:], start=True, stop=True)
 
-        for piece in range(pieces):
-            first = piece * PIECE
-            bank = banks.tile([P, PIECE], F32, name="bank")
-            picked = tokens[:].indirect(
-                offsets[:, first // PER_COLUMN : (first + PIECE) // PER_COLUMN]
-            )
-            nc.tensor.matmul(bank[:], weights[:], picked, start=True, stop=True)
-
-            result = results.tile([P, PIECE], F32, name="result")
-            if piece % 2 == 0:
-                nc.scalar.activation(result[:], bank[:], RELU, bias=bias[:, 0:1])
-            else:
-                nc.vector.tensor_scalar(result[:], bank[:], bias[:, 0:1], 0.0, ADD, MAX)
-            nc.sync.dma_start(out[:, first : first + PIECE], result[:])
+        for store in range(TOKENS // STORE):
+            result = results.tile([P, STORE], F32, name="result")
+            for side in range(2):
+                first = store * STORE + side * PIECE
+                bank = banks.tile([P, PIECE], F32, name="bank")
+                picked = tokens[:].indirect(
+                    offsets[:, first // PER_COLUMN : (first + PIECE) // PER_COLUMN]
+                )
+                nc.tensor.matmul(bank[:], weights[:], picked, start=True, stop=True)
+                if side == 0:
+                    nc.scalar.activation(result[:, 0:PIECE], bank[:], RELU, bias=bias[:, 0:1])
+                else:
+                    nc.vector.tensor_scalar(
+                        result[:, PIECE:STORE], bank[:], bias[:, 0:1], 0.0, ADD, MAX
+                    )
+            nc.sync.dma_start(out[:, store * STORE : (store + 1) * STORE], result[:])

@@ -6,8 +6,7 @@ ADD, MAX = mybir.AluOpType.add, mybir.AluOpType.max
 
 P = 128
 TOKENS = 2048
-PIECE = 128
-STORE = 2 * PIECE
+STORE = 256
 PER_COLUMN = 16
 BANKS = 7
 WARM_UPS = 16
@@ -43,19 +42,27 @@ def tile_gather_matmul_kernel(tc, table, w, b, offs, out):
         for turn in range(WARM_UPS):
             nc.tensor.matmul(unused[:], zeros[:], zeros[:], start=True, stop=True)
 
-        for store in range(TOKENS // STORE):
+        stores = TOKENS // STORE
+        piece = 0
+        for store in range(stores):
+            at_an_end = store == 0 or store == stores - 1
+            width = STORE // 2 if at_an_end else STORE
             result = results.tile([P, STORE], F32, name="result")
-            for side in range(2):
-                first = store * STORE + side * PIECE
-                bank = banks.tile([P, PIECE], F32, name="bank")
+            for left in range(0, STORE, width):
+                first = store * STORE + left
+                bank = banks.tile([P, width], F32, name="bank")
                 picked = tokens[:].indirect(
-                    offsets[:, first // PER_COLUMN : (first + PIECE) // PER_COLUMN]
+                    offsets[:, first // PER_COLUMN : (first + width) // PER_COLUMN]
                 )
                 nc.tensor.matmul(bank[:], weights[:], picked, start=True, stop=True)
-                if side == 0:
-                    nc.scalar.activation(result[:, 0:PIECE], bank[:], RELU, bias=bias[:, 0:1])
+
+                if piece % 2 == 0:
+                    nc.scalar.activation(
+                        result[:, left : left + width], bank[:], RELU, bias=bias[:, 0:1]
+                    )
                 else:
                     nc.vector.tensor_scalar(
-                        result[:, PIECE:STORE], bank[:], bias[:, 0:1], 0.0, ADD, MAX
+                        result[:, left : left + width], bank[:], bias[:, 0:1], 0.0, ADD, MAX
                     )
+                piece += 1
             nc.sync.dma_start(out[:, store * STORE : (store + 1) * STORE], result[:])

@@ -8,8 +8,7 @@ P = 128
 TOKENS = 2048
 STORE = 256
 PER_COLUMN = 16
-BANKS = 7
-WARM_UPS = 16
+BANKS = 8
 
 FLOPS = 2 * P * P * TOKENS
 
@@ -20,7 +19,6 @@ def tile_gather_matmul_kernel(tc, table, w, b, offs, out):
     with (
         tc.tile_pool(name="held", bufs=1) as held,
         tc.tile_pool(name="results", bufs=TOKENS // STORE) as results,
-        tc.psum_pool(name="idle_bank", bufs=1) as idle_bank,
         tc.psum_pool(name="banks", bufs=BANKS) as banks,
     ):
         offsets = held.tile([P, TOKENS // PER_COLUMN], U16, name="offsets")
@@ -33,14 +31,10 @@ def tile_gather_matmul_kernel(tc, table, w, b, offs, out):
         nc.sync.dma_start(tokens[:, half:TOKENS], table[:, half:TOKENS])
         nc.scalar.dma_start(bias[:], b)
 
-        zeros = held.tile([P, P], BF16, name="zeros")
-        nc.gpsimd.memset(zeros[:], 0.0)
+        zeros = held.tile([P, 1], BF16, name="zeros")
+        nc.vector.memset(zeros[:], 0.0)
         early = held.tile([P, 1], BF16, name="early")
-        nc.scalar.activation(early[:], zeros[:, 0:1], RELU)
-
-        unused = idle_bank.tile([P, P], F32, name="unused")
-        for turn in range(WARM_UPS):
-            nc.tensor.matmul(unused[:], zeros[:], zeros[:], start=True, stop=True)
+        nc.scalar.activation(early[:], zeros[:], RELU)
 
         stores = TOKENS // STORE
         piece = 0

import concourse.mybir as mybir

BF16, F32, U16 = mybir.dt.bfloat16, mybir.dt.float32, mybir.dt.uint16
RELU = mybir.ActivationFunctionType.Relu
ADD, MAX = mybir.AluOpType.add, mybir.AluOpType.max

P = 128
TOKENS = 2048
STORE = 256
PER_COLUMN = 16
BANKS = 8

FLOPS = 2 * P * P * TOKENS


def tile_gather_matmul_kernel(tc, table, w, b, offs, out):
    nc = tc.nc
    half = TOKENS // 2
    with (
        tc.tile_pool(name="held", bufs=1) as held,
        tc.tile_pool(name="results", bufs=TOKENS // STORE) as results,
        tc.psum_pool(name="banks", bufs=BANKS) as banks,
    ):
        offsets = held.tile([P, TOKENS // PER_COLUMN], U16, name="offsets")
        tokens = held.tile([P, TOKENS], BF16, name="tokens")
        weights = held.tile([P, P], BF16, name="weights")
        bias = held.tile([P, 1], F32, name="bias")
        nc.sync.dma_start(offsets[:], offs)
        nc.scalar.dma_start(tokens[:, 0:half], table[:, 0:half])
        nc.sync.dma_start(weights[:], w)
        nc.sync.dma_start(tokens[:, half:TOKENS], table[:, half:TOKENS])
        nc.scalar.dma_start(bias[:], b)

        zeros = held.tile([P, 1], BF16, name="zeros")
        nc.vector.memset(zeros[:], 0.0)
        early = held.tile([P, 1], BF16, name="early")
        nc.scalar.activation(early[:], zeros[:], RELU)

        stores = TOKENS // STORE
        piece = 0
        for store in range(stores):
            at_an_end = store == 0 or store == stores - 1
            width = STORE // 2 if at_an_end else STORE
            result = results.tile([P, STORE], F32, name="result")
            for left in range(0, STORE, width):
                first = store * STORE + left
                bank = banks.tile([P, width], F32, name="bank")
                picked = tokens[:].indirect(
                    offsets[:, first // PER_COLUMN : (first + width) // PER_COLUMN]
                )
                nc.tensor.matmul(bank[:], weights[:], picked, start=True, stop=True)

                if piece % 2 == 0:
                    nc.scalar.activation(
                        result[:, left : left + width], bank[:], RELU, bias=bias[:, 0:1]
                    )
                else:
                    nc.vector.tensor_scalar(
                        result[:, left : left + width], bank[:], bias[:, 0:1], 0.0, ADD, MAX
                    )
                piece += 1
            nc.sync.dma_start(out[:, store * STORE : (store + 1) * STORE], result[:])
